import numpy as np
import ml_dtypes


def mxq(x, axis, fmt="e4m3"):
    dtype, down = {"e4m3": (ml_dtypes.float8_e4m3fn, 7), "e5m2": (ml_dtypes.float8_e5m2, 14)}[fmt]
    v = np.moveaxis(np.asarray(x, np.float32).astype(ml_dtypes.bfloat16).astype(np.float64), axis, -1)
    blocks = v.reshape(v.shape[:-1] + (-1, 32))
    amax = np.abs(blocks).max(-1, keepdims=True)
    byte = np.maximum(np.where(amax > 0, np.frexp(amax)[1] - 1 + 127, 0) - down, 1)
    scale = np.exp2(byte - 127.0)
    codes = (blocks / scale).astype(np.float32).astype(dtype).astype(np.float64)
    return np.moveaxis((codes * scale).reshape(v.shape), -1, axis)


WIDE = False


def mx_kscale(k):
    if not WIDE:
        return np.ones(k)
    levels = np.array([10, -10, 5, -5, 0])
    if k % 512:
        return np.exp2(np.random.permutation(np.resize(levels, k // 32))).repeat(32)
    a = np.empty((k // 512, 16))
    for p in range(k // 512):
        a[p, :8] = np.random.permutation(np.resize(levels, 8))
        for g in range(8):
            far = levels[np.abs(levels - a[p, g]) >= 10]
            a[p, g + 8] = far[np.random.randint(len(far))]
    return np.exp2(a.ravel()).repeat(32)


def f64(x):
    return np.asarray(x).astype(np.float64)


def striped(idx):
    return np.tile(idx.reshape(-1, 16).T, (8, 1)).astype(np.uint16)


def unstriped(offs):
    return offs[:16].T.reshape(-1).astype(np.int64)


E2M1 = np.array([0.0, 0.5, 1.0, 1.5, 2.0, 3.0, 4.0, 6.0, -0.0, -0.5, -1.0, -1.5, -2.0, -3.0, -4.0, -6.0])


def pack_weight(w, fmt):
    k, n = w.shape
    w = f64(np.asarray(w, np.float32).astype(ml_dtypes.bfloat16)).reshape(k // 32, 32, n)
    amax = np.abs(w).max(1)
    if fmt == "e4m3":
        byte = np.frexp(amax)[1] - 1 + 127 - 7
    else:
        mant, ex = np.frexp(amax / 6.0)
        byte = np.where(mant > 0.5, ex, ex - 1) + 127
    byte = np.clip(np.where(amax > 0, byte, 1), 1, 254)
    scaled = (w * np.exp2(127.0 - byte)[:, None, :]).reshape(k, n).astype(np.float32)
    by_word = np.ascontiguousarray(scaled.reshape(k // 512, 128, 4, n).transpose(0, 1, 3, 2))
    if fmt == "e4m3":
        words = by_word.astype(ml_dtypes.float8_e4m3fn).view(np.uint8)
    else:
        c = by_word.astype(ml_dtypes.float4_e2m1fn).view(np.uint8) & 0xF
        words = (c[..., 0::2] | (c[..., 1::2] << 4)).reshape(k // 512, 128, 2 * n)
    return np.ascontiguousarray(words), np.ascontiguousarray(byte.astype(np.uint8).reshape(k // 512, 16, n))


def unpack_weight(words, scales, fmt):
    g, _, n = scales.shape
    words = np.ascontiguousarray(words).reshape(g, 128, n, -1)
    if fmt == "e4m3":
        vals = words.view(ml_dtypes.float8_e4m3fn).astype(np.float64)
    else:
        nib = np.empty((g, 128, n, 4), np.uint8)
        nib[..., 0::2] = words & 0xF
        nib[..., 1::2] = words >> 4
        vals = E2M1[nib]
    vals = vals * np.repeat(np.exp2(scales.astype(np.float64) - 127.0), 8, axis=1)[..., None]
    return vals.transpose(0, 1, 3, 2).reshape(g * 512, n)


def gelu(v):
    return 0.5 * v * (1.0 + np.tanh(np.sqrt(2.0 / np.pi) * (v + 0.044715 * v**3)))


K, K2, T, S, H, T2, P, N = 1024, 512, 2048, 512, 1024, 2048, 1024, 512

def setup_inputs():
    n = np.random.standard_normal
    s, s2, u = mx_kscale(K)[:, None], mx_kscale(K2)[:, None], mx_kscale(H)[:, None]
    d = {}
    d["tab_words"], d["tab_scales"] = pack_weight(n((K, T)) * s, "e4m3")
    d["offs"] = striped(np.random.permutation(T)[:S])
    d["tab2_words"], d["tab2_scales"] = pack_weight(n((K2, T)) * s2, "e4m3")
    d["offs2"] = striped(np.random.permutation(T)[:S])
    d["w1"] = (0.8 * n((K, H)) / K ** 0.5 / s).astype(np.float32)
    d["w2_words"], d["w2_scales"] = pack_weight(0.9 * n((K, H)) / K ** 0.5 / s, "e2m1")
    d["w3"] = (0.95 * n((K2, H)) / K2 ** 0.5 / s2).astype(np.float32)
    d["page0"] = (1.2 * n((H, T2))).astype(np.float32)
    perm = np.random.permutation(T2)
    d["offs3"], d["offs4"] = striped(perm[:S]), striped(perm[S:2 * S])
    d["wg1"] = np.exp(0.3 * n((128, S))).astype(np.float32)
    d["wg2"] = np.exp(0.3 * n((128, S))).astype(np.float32)
    d["offs5"] = striped(np.random.permutation(T2)[:P])
    d["vec"] = (0.8 * n(H) - 0.3).astype(np.float32)
    d["gain"] = (np.exp(0.3 * n(H)) * u[:, 0]).astype(np.float32)
    d["w4_words"], d["w4_scales"] = pack_weight(1.5 * n((H, N)) / H ** 0.5 / u, "e2m1")
    return d

def reference(tab_words, tab_scales, offs, tab2_words, tab2_scales, offs2, w1, w2_words, w2_scales,
              w3, page0, offs3, offs4, wg1, wg2, offs5, vec, gain, w4_words, w4_scales):
    v = unpack_weight(tab_words, tab_scales, "e4m3")[:, unstriped(offs)]
    v2 = unpack_weight(tab2_words, tab2_scales, "e4m3")[:, unstriped(offs2)]
    a = mxq(f64(w1), 0, "e4m3").T @ v
    b = unpack_weight(w2_words, w2_scales, "e2m1").T @ v
    h1 = a * b + a
    c = mxq(f64(w3), 0, "e4m3").T @ v2
    h2 = np.square(c)
    page = f64(page0).copy()
    page[:, unstriped(offs3)] = np.tile(f64(wg1), (H // 128, 1)) * h1
    page[:, unstriped(offs4)] = np.tile(f64(wg2), (H // 128, 1)) * h2
    x = f64(gain)[:, None] * np.tanh(page[:, unstriped(offs5)] + f64(vec)[:, None])
    y = unpack_weight(w4_words, w4_scales, "e2m1").T @ mxq(x, 0, "e4m3")
    return np.abs(y)

@@ -1,0 +1,338 @@
+from contextlib import ExitStack
+
+import concourse.mybir as mybir
+
+K, K2, T, S, H, T2, PICK, N = 1024, 512, 2048, 512, 1024, 2048, 1024, 512
+FLOPS = 2 * (K * H * S * 2 + K2 * H * S + H * N * PICK)
+
+F32, BF16 = mybir.dt.float32, mybir.dt.bfloat16
+I32, U32, U16, U8 = mybir.dt.int32, mybir.dt.uint32, mybir.dt.uint16, mybir.dt.uint8
+FP8X4, FP4X4 = mybir.dt.float8_e4m3fn_x4, mybir.dt.float4_e2m1fn_x4
+MULT = mybir.AluOpType.mult
+ACT = mybir.ActivationFunctionType
+
+P = 128
+PACK = 4
+PASS = P * PACK
+CHUNK = 256
+NSUB = 128
+
+
+def tile_list_fencing_referee_features_kernel(
+    tc, tab_words, tab_scales, offs, tab2_words, tab2_scales, offs2, w1, w2_words, w2_scales,
+    w3, page0, offs3, offs4, wg1, wg2, offs5, vec, gain, w4_words, w4_scales, out,
+):
+    nc = tc.nc
+    with ExitStack() as ctx:
+        lists = ctx.enter_context(tc.tile_pool(name="lists", bufs=1))
+        sb = ctx.enter_context(tc.tile_pool(name="sb", bufs=1))
+        psum = ctx.enter_context(tc.psum_pool(name="psum", bufs=1))
+
+        def tile(name, shape, dtype, tag=None):
+            return sb.tile(shape, dtype, name=name, tag=tag or name, align_bytes=64)
+
+        def load_list(name, src):
+            dst = lists.tile(list(src.shape), U16, name=name, tag=name)
+            nc.sync.dma_start(dst[:], src)
+            return dst
+
+        banks_used = []
+
+        def next_bank():
+            n = len(banks_used)
+            bank = psum.tile([P, 512], F32, name="bank%d" % n, tag="bank%d" % (n % 8))
+            banks_used.append(bank)
+            return bank
+
+        def load_scale_rows(name, src, queues=(nc.sync, nc.sync)):
+            passes, width = src.shape[0], src.shape[2]
+            dst = tile(name, [P, passes * width], U8)
+            nc.vector.memset(dst[:].bitcast(I32), 0)
+            for q in range(4):
+                queues[q % 2].dma_start(
+                    out=dst[32 * q : 32 * q + 4, :].bitcast(I32).rearrange("p (a c) -> p a c", a=passes),
+                    in_=src[:, 4 * q : 4 * q + 4, :].bitcast(I32).rearrange("a q c -> q a c"),
+                )
+            return dst
+
+        def load_table_words(name, src):
+            dst = tile(name, [P, T], I32)
+            nc.sync.dma_start(out=dst[:], in_=src.rearrange("p t i -> p (t i)").bitcast(I32))
+            return dst
+
+        def load_packed_words(name, src, tag=None):
+            passes, width = src.shape[0], src.shape[2]
+            dst = tile(name, [P, passes * width], U8, tag)
+            nc.sync.dma_start(
+                out=dst[:].bitcast(I32).rearrange("p (a c) -> p a c", a=passes),
+                in_=src.bitcast(I32).rearrange("a p c -> p a c"),
+            )
+            return dst
+
+        def load_weight(name, src, a, b, tag):
+            dst = tile(name, [P, PACK, PASS], F32, tag)
+            block = src[a * PASS : (a + 1) * PASS, b * PASS : (b + 1) * PASS]
+            nc.sync.dma_start(out=dst[:], in_=block.rearrange("(p j) c -> p j c", j=PACK))
+            return dst
+
+        def load_page(i):
+            b, t = divmod(i, PACK)
+            dst = tile("page%d" % i, [P, T2], F32)
+            rows = page0[b * PASS : (b + 1) * PASS, :].rearrange("(p t) c -> t p c", t=PACK)
+            nc.sync.dma_start(out=dst[:], in_=rows[t])
+            return dst
+
+        def load_gate(dst, src, t0, t1):
+            rows = src.rearrange("(q t) j -> q t j", t=PACK)
+            for quadrant in (0, 2, 1, 3):
+                nc.sync.dma_start(out=dst[32 * quadrant : 32 * quadrant + 32, t0:t1, :], in_=rows[:, t0:t1, :])
+
+        def load_columns(name, src):
+            dst = tile(name, [P, 2, PACK], F32)
+            nc.sync.dma_start(out=dst[:], in_=src.rearrange("(b p t) -> p b t", b=2, t=PACK))
+            return dst[:].rearrange("p b t -> p (b t)")
+
+        def gather_words(name, window, offsets):
+            dst = tile(name, [P, S], U32)
+            nc.vector.tensor_copy(dst[:], window[:].bitcast(U32).indirect(offsets[:]))
+            return dst
+
+        def gather_scales(name, window, a, offsets):
+            dst = tile(name, [P, S], U8)
+            nc.vector.tensor_copy(dst[:], window[:, a * T : (a + 1) * T].indirect(offsets[:]))
+            return dst
+
+        def round_weight(name, raw, tag):
+            dst = tile(name, [P, PACK * PASS], BF16, tag)
+            nc.scalar.copy(
+                dst[:].rearrange("p (t m j) -> p m j t", t=PACK, j=PACK),
+                raw[:].rearrange("p j (m t) -> p m j t", t=PACK),
+            )
+            return dst
+
+        def quantize(name, src, tag=None):
+            width = src.shape[1] // PACK
+            codes = tile(name + "_codes", [P, width], U32, tag)
+            scales = tile(name + "_scales", [P, width], U8)
+            nc.vector.quantize_mx(out=codes[:].bitcast(FP8X4), scales=scales[:], in_=src[:])
+            return codes, scales
+
+        def fp8_cols(pair, c0, width):
+            return pair[0][:, c0 : c0 + width].bitcast(FP8X4), pair[1][:, c0 : c0 + width]
+
+        def fp4_cols(pair, c0, width):
+            return pair[0][:, 2 * c0 : 2 * (c0 + width)].bitcast(FP4X4), pair[1][:, c0 : c0 + width]
+
+        def mx(dst, lhs, rhs, start, stop):
+            nc.tensor.matmul_mx(out=dst, lhsT=lhs[0], lhsT_scale=lhs[1], rhs=rhs[0], rhs_scale=rhs[1], start=start, stop=stop)
+
+
+        pages = [None] * 8
+        wg1_sb = tile("wg1_sb", [P, PACK, S], F32)
+        wg2_sb = tile("wg2_sb", [P, PACK, S], F32, "wg2")
+        idx2 = load_list("idx2", offs2)
+        w3_raw0 = load_weight("w3_raw0", w3, 0, 0, "stage0")
+        tab2_s = load_scale_rows("tab2_s", tab2_scales, (nc.sync, nc.scalar))
+        tab2_w = load_table_words("tab2_w", tab2_words[0])
+        w2_w_raw = load_packed_words("w2_w_raw", w2_words, "bent")
+        idx4 = load_list("idx4", offs4)
+        pages[0] = load_page(0)
+        load_gate(wg2_sb, wg2, 0, 1)
+        pages[1] = load_page(1)
+        load_gate(wg2_sb, wg2, 1, 3)
+        pages[2] = load_page(2)
+        w2_s_raw = load_scale_rows("w2_s_raw", w2_scales)
+        w3_raw1 = load_weight("w3_raw1", w3, 0, 1, "stage1")
+        pages[3] = load_page(3)
+        load_gate(wg2_sb, wg2, 3, 4)
+        pages[4] = load_page(4)
+        idx = load_list("idx", offs)
+        tab_s = load_scale_rows("tab_s", tab_scales)
+        tab_w0 = load_table_words("tab_w0", tab_words[0])
+        tab_w1 = load_table_words("tab_w1", tab_words[1])
+        w1_raw00 = load_weight("w1_raw00", w1, 0, 0, "stage2")
+        pages[5] = load_page(5)
+        w1_raw10 = load_weight("w1_raw10", w1, 1, 0, "stage3")
+        pages[6] = load_page(6)
+        idx3 = load_list("idx3", offs3)
+        load_gate(wg1_sb, wg1, 0, 2)
+        pages[7] = load_page(7)
+        idx5 = load_list("idx5", offs5)
+        vec_sb = load_columns("vec_sb", vec)
+        gain_sb = load_columns("gain_sb", gain)
+        load_gate(wg1_sb, wg1, 2, 4)
+
+        v2 = (None, gather_scales("v2_s", tab2_s, 0, idx2))
+        v2 = (gather_words("v2_w", tab2_w, idx2), v2[1])
+        w3_q = [quantize("w3_q0", round_weight("w3_r0", w3_raw0, "round0"), "codes0")]
+
+        w2_w = tile("w2_w", [P, 2 * 2 * H], U8)
+        nc.vector.tensor_copy(
+            w2_w[:].bitcast(U16).rearrange("p (g t q) -> p g t q", t=PACK, q=P),
+            w2_w_raw[:].bitcast(U16).rearrange("p (g q t) -> p g t q", t=PACK, q=P),
+        )
+        w2_s = tile("w2_s", [P, 2 * H], U8)
+        nc.vector.tensor_copy(
+            w2_s[:].rearrange("p (g t q) -> p g t q", t=PACK, q=P),
+            w2_s_raw[:].rearrange("p (g q t) -> p g t q", t=PACK, q=P),
+        )
+
+        def put_right(i):
+            b, t = divmod(i, PACK)
+            bank = next_bank()
+            mx(bank[:], fp8_cols(w3_q[b], t * P, P), fp8_cols(v2, 0, S), True, True)
+            h2 = tile("h2_%d" % i, [P, S], F32, "small%d" % t)
+            nc.scalar.activation(h2[:], bank[:], ACT.Square)
+            nc.vector.tensor_tensor(pages[i][:].indirect(idx4[:]), h2[:], wg2_sb[:, t, :], MULT)
+
+        for i in range(3):
+            put_right(i)
+        w3_q.append(quantize("w3_q1", round_weight("w3_r1", w3_raw1, "round1"), "codes1"))
+        w1_raw01 = load_weight("w1_raw01", w1, 0, 1, "stage0")
+        w1_raw11 = load_weight("w1_raw11", w1, 1, 1, "stage1")
+        w4_s = load_scale_rows("w4_s", w4_scales)
+        w4_w = load_packed_words("w4_w", w4_words)
+        put_right(3)
+        put_right(4)
+        v = [(gather_words("v_w0", tab_w0, idx), gather_scales("v_s0", tab_s, 0, idx))]
+        v.append((gather_words("v_w1", tab_w1, idx), gather_scales("v_s1", tab_s, 1, idx)))
+        put_right(5)
+        w1_q = {}
+        w1_q[0, 0] = quantize("w1_q00", round_weight("w1_r00", w1_raw00, "round0"), "codes2")
+        put_right(6)
+        w1_q[1, 0] = quantize("w1_q10", round_weight("w1_r10", w1_raw10, "round1"), "codes3")
+        put_right(7)
+
+        left2_all = [tile("left2_b%d" % b, [P, PACK, S], F32, ["stage3", "stage2"][b]) for b in range(2)]
+
+        def left_products(pair):
+            left = tile("left%d" % pair, [P, 2, S], F32, "left%d" % pair)
+            left2 = left2_all[pair // 2][:, 2 * (pair % 2) : 2 * (pair % 2) + 2, :]
+            for u in range(2):
+                b, t = divmod(2 * pair + u, PACK)
+                bank = next_bank()
+                for a in range(2):
+                    mx(bank[:], fp8_cols(w1_q[a, b], t * P, P), fp8_cols(v[a], 0, S), a == 0, a == 1)
+                nc.scalar.copy(left[:, u, :], bank[:])
+                bank = next_bank()
+                for a in range(2):
+                    mx(bank[:], fp4_cols((w2_w, w2_s), a * H + b * PASS + t * P, P), fp8_cols(v[a], 0, S), a == 0, a == 1)
+                nc.scalar.activation(left2[:, u, :], bank[:], ACT.Identity, bias=1.0)
+            return left, left2
+
+        def left_features(pair):
+            left, left2 = products[pair]
+            nc.vector.tensor_tensor(left[:], left[:], left2, MULT)
+
+        def put_left(i, h1):
+            nc.vector.tensor_tensor(pages[i][:].indirect(idx3[:]), h1, wg1_sb[:, i % PACK, :], MULT)
+
+        def put_pair(pair):
+            for u in range(2):
+                put_left(2 * pair + u, products[pair][0][:, u, :])
+
+        got_tag = ["got0", "got1", "stage1", "round1", "stage0", "left0", "left1", "got0"]
+        x_rows = [tile("x_rows0", [P, PACK, PICK], BF16), None]
+        chunks = PICK // CHUNK
+
+        def fetch(i):
+            got = tile("got%d" % i, [P, PICK], F32, got_tag[i])
+            nc.vector.tensor_copy(got[:], pages[i][:].indirect(idx5[:]))
+            bent = tile("bent%d" % i, [P, PICK], F32, "bent")
+            nc.scalar.activation(bent[:], got[:], ACT.Tanh, bias=vec_sb[:, i : i + 1])
+            return bent
+
+        def fetch_rows(i):
+            b, t = divmod(i, PACK)
+            nc.scalar.activation(x_rows[b][:, t, :], fetch(i)[:], ACT.Copy, scale=gain_sb[:, i : i + 1])
+
+        products = [left_products(0), left_products(1)]
+        left_features(0)
+        put_pair(0)
+        left_features(1)
+        fetch_rows(0)
+        fetch_rows(1)
+        put_pair(1)
+        w1_q[0, 1] = quantize("w1_q01", round_weight("w1_r01", w1_raw01, "round0"), "codes4")
+        w1_q[1, 1] = quantize("w1_q11", round_weight("w1_r11", w1_raw11, "round1"), "codes5")
+        products.append(left_products(2))
+        products.append(left_products(3))
+        fetch_rows(2)
+        fetch_rows(3)
+        woven = []
+        for half in range(2):
+            dst = tile("x_woven0%d" % half, [P, PACK * 512], BF16, "round%d" % half)
+            nc.scalar.copy(
+                dst[:].rearrange("p (c i t) -> p c t i", i=4, t=PACK),
+                x_rows[0][:, :, half * 512 : (half + 1) * 512].rearrange("p t (c i) -> p c t i", i=4),
+            )
+            woven.append(dst)
+        left_features(2)
+        put_pair(2)
+        x_rows[1] = tile("x_rows1", [P, 2, PICK], BF16, "wg2")
+        fetch_rows(4)
+        fetch_rows(5)
+        woven1 = [tile("x_woven1%d" % c, [P, PACK * CHUNK], BF16, "small%d" % c) for c in range(chunks)]
+        for c in range(chunks):
+            nc.scalar.copy(
+                woven1[c][:].rearrange("p (j t) -> p j t", t=PACK)[:, :, 0:2],
+                x_rows[1][:, :, c * CHUNK : (c + 1) * CHUNK].rearrange("p t j -> p j t"),
+            )
+        left, left2 = products[3]
+        nc.vector.tensor_tensor(left[:, 0, :], left[:, 0, :], left2[:, 0, :], MULT)
+        put_left(6, left[:, 0, :])
+        got6 = fetch(6)
+        for c in range(chunks):
+            nc.scalar.activation(
+                woven1[c][:].rearrange("p (j t) -> p j t", t=PACK)[:, :, 2],
+                got6[:, c * CHUNK : (c + 1) * CHUNK], ACT.Copy, scale=gain_sb[:, 6:7],
+            )
+        x_q0 = [quantize("x_q00", woven[0], "codes0")]
+        h1_last = tile("h1_last", [P, S], F32, "round0")
+        nc.vector.tensor_tensor(h1_last[:], left[:, 1, :], left2[:, 1, :], MULT)
+        put_left(7, h1_last[:])
+        x_q0.append(quantize("x_q01", woven[1], "codes1"))
+
+        def out_passes(chunk, a, x_pair, c0):
+            for nt in range(N // P):
+                bank = out_banks[2 * chunk + nt // 2]
+                for s in range(CHUNK // NSUB):
+                    col = (nt % 2) * CHUNK + s * NSUB
+                    first = a == 0 and col == 0
+                    last = a == 1 and col == 512 - NSUB
+                    mx(bank[:, col : col + NSUB], fp4_cols((w4_w, w4_s), a * N + nt * P, P), fp8_cols(x_pair, c0 + s * NSUB, NSUB), first, last)
+
+        out_banks = [next_bank() for c in range(2 * chunks)]
+        for c in range(chunks):
+            out_passes(c, 0, x_q0[c // 2], (c % 2) * CHUNK)
+
+        got = tile("got7", [P, PICK], F32, got_tag[7])
+        bent_last = tile("bent7", [P, PICK], F32, "bent")
+
+        def fetch_last(c):
+            cols = slice(c * CHUNK, (c + 1) * CHUNK)
+            nc.vector.tensor_copy(got[:, cols], pages[7][:].indirect(idx5[:, c * CHUNK // 16 : (c + 1) * CHUNK // 16]))
+            nc.scalar.activation(bent_last[:, cols], got[:, cols], ACT.Tanh, bias=vec_sb[:, 7:8])
+
+        def gain_last(c):
+            nc.vector.tensor_scalar(
+                woven1[c][:].rearrange("p (j t) -> p j t", t=PACK)[:, :, 3],
+                bent_last[:, c * CHUNK : (c + 1) * CHUNK], gain_sb[:, 7:8], None, MULT,
+            )
+
+        def finish(c):
+            x_pair = quantize("x_q1%d" % c, woven1[c], "codes%d" % (2 + c))
+            out_passes(c, 1, x_pair, 0)
+            staged = tile("staged%d" % c, [P, N // P, CHUNK], F32, ["stage0", "stage1", "stage3", "got1"][c])
+            for h in range(2):
+                bank = out_banks[2 * c + h]
+                nc.scalar.activation(staged[:, 2 * h : 2 * h + 2, :].rearrange("p n j -> p (n j)"), bank[:], ACT.Abs)
+                rows = out[2 * h * P : (2 * h + 2) * P, c * CHUNK : (c + 1) * CHUNK]
+                nc.sync.dma_start(out=rows.rearrange("(n p) j -> p n j", p=P), in_=staged[:, 2 * h : 2 * h + 2, :])
+
+        steps = (fetch_last, gain_last, finish)
+        for tick in range(chunks + len(steps) - 1):
+            for depth in range(len(steps)):
+                c = tick - depth
+                if 0 <= c < chunks:
+                    steps[depth](c)

@@ -1,6 +1,7 @@
 from contextlib import ExitStack
 
 import concourse.mybir as mybir
+from concourse.masks import make_identity
 
 K, K2, T, S, H, T2, PICK, N = 1024, 512, 2048, 512, 1024, 2048, 1024, 512
 FLOPS = 2 * (K * H * S * 2 + K2 * H * S + H * N * PICK)
@@ -38,9 +39,9 @@ def tile_list_fencing_referee_features_kernel(
 
         banks_used = []
 
-        def next_bank():
+        def next_bank(slot=None):
             n = len(banks_used)
-            bank = psum.tile([P, 512], F32, name="bank%d" % n, tag="bank%d" % (n % 8))
+            bank = psum.tile([P, 512], F32, name="bank%d" % n, tag="bank%d" % (n % 8 if slot is None else slot))
             banks_used.append(bank)
             return bank
 
@@ -53,6 +54,13 @@ def tile_list_fencing_referee_features_kernel(
                     out=dst[32 * q : 32 * q + 4, :].bitcast(I32).rearrange("p (a c) -> p a c", a=passes),
                     in_=src[:, 4 * q : 4 * q + 4, :].bitcast(I32).rearrange("a q c -> q a c"),
                 )
+            return dst
+
+        def load_packed_scale_rows(name, src):
+            dst = tile(name, [P, T], U8)
+            nc.vector.memset(dst[:].bitcast(I32), 0)
+            for q in range(4):
+                nc.sync.dma_start(out=dst[32 * q : 32 * q + 8, :].bitcast(I32), in_=src[:, 4 * q : 4 * q + 4, :].bitcast(I32))
             return dst
 
         def load_table_words(name, src):
@@ -82,10 +90,25 @@ def tile_list_fencing_referee_features_kernel(
             nc.sync.dma_start(out=dst[:], in_=rows[t])
             return dst
 
-        def load_gate(dst, src, t0, t1):
-            rows = src.rearrange("(q t) j -> q t j", t=PACK)
-            for quadrant in (0, 2, 1, 3):
-                nc.sync.dma_start(out=dst[32 * quadrant : 32 * quadrant + 32, t0:t1, :], in_=rows[:, t0:t1, :])
+        def load_gate(name, src, tag):
+            dst = tile(name, [P, S], F32, tag)
+            nc.sync.dma_start(out=dst[:], in_=src)
+            return dst
+
+        def turn_gate(name, rows, tag, copy, slot):
+            bank = next_bank(slot)
+            for jb in range(S // P):
+                nc.tensor.transpose(bank[:, jb * P : (jb + 1) * P], rows[:, jb * P : (jb + 1) * P], ident[:])
+            turned = tile(name, [P, S // P, PACK * P], F32, tag)
+            for rep in range(PACK):
+                copy(turned[:, :, rep * P : (rep + 1) * P], bank[:].rearrange("p (b r) -> p b r", r=P))
+            return turned
+
+        def deal_gate(dst, turned, t, slot=None):
+            bank = next_bank(slot)
+            for jb in range(S // P):
+                nc.tensor.transpose(bank[:, jb * P : (jb + 1) * P], turned[:, jb, t :: PACK], ident[:])
+            nc.scalar.copy(dst[:, t, :], bank[:])
 
         def load_columns(name, src):
             dst = tile(name, [P, 2, PACK], F32)
@@ -104,9 +127,10 @@ def tile_list_fencing_referee_features_kernel(
 
         def round_weight(name, raw, tag):
             dst = tile(name, [P, PACK * PASS], BF16, tag)
-            nc.scalar.copy(
+            nc.scalar.activation(
                 dst[:].rearrange("p (t m j) -> p m j t", t=PACK, j=PACK),
                 raw[:].rearrange("p j (m t) -> p m j t", t=PACK),
+                ACT.Copy,
             )
             return dst
 
@@ -130,6 +154,9 @@ def tile_list_fencing_referee_features_kernel(
         pages = [None] * 8
         wg1_sb = tile("wg1_sb", [P, PACK, S], F32)
         wg2_sb = tile("wg2_sb", [P, PACK, S], F32, "wg2")
+        ident = tile("ident", [P, P], F32)
+        make_identity(nc, ident[:])
+        wg2_rows = load_gate("wg2_rows", wg2, "got0")
         idx2 = load_list("idx2", offs2)
         w3_raw0 = load_weight("w3_raw0", w3, 0, 0, "stage0")
         tab2_s = load_scale_rows("tab2_s", tab2_scales, (nc.sync, nc.scalar))
@@ -137,31 +164,29 @@ def tile_list_fencing_referee_features_kernel(
         w2_w_raw = load_packed_words("w2_w_raw", w2_words, "bent")
         idx4 = load_list("idx4", offs4)
         pages[0] = load_page(0)
-        load_gate(wg2_sb, wg2, 0, 1)
         pages[1] = load_page(1)
-        load_gate(wg2_sb, wg2, 1, 3)
         pages[2] = load_page(2)
-        w2_s_raw = load_scale_rows("w2_s_raw", w2_scales)
         w3_raw1 = load_weight("w3_raw1", w3, 0, 1, "stage1")
+        wg1_rows = load_gate("wg1_rows", wg1, "got1")
         pages[3] = load_page(3)
-        load_gate(wg2_sb, wg2, 3, 4)
+        w2_s_raw = load_scale_rows("w2_s_raw", w2_scales)
         pages[4] = load_page(4)
         idx = load_list("idx", offs)
-        tab_s = load_scale_rows("tab_s", tab_scales)
+        tab_s = load_packed_scale_rows("tab_s", tab_scales)
         tab_w0 = load_table_words("tab_w0", tab_words[0])
-        tab_w1 = load_table_words("tab_w1", tab_words[1])
         w1_raw00 = load_weight("w1_raw00", w1, 0, 0, "stage2")
         pages[5] = load_page(5)
         w1_raw10 = load_weight("w1_raw10", w1, 1, 0, "stage3")
-        pages[6] = load_page(6)
+        tab_w1 = load_table_words("tab_w1", tab_words[1])
         idx3 = load_list("idx3", offs3)
-        load_gate(wg1_sb, wg1, 0, 2)
+        pages[6] = load_page(6)
         pages[7] = load_page(7)
         idx5 = load_list("idx5", offs5)
         vec_sb = load_columns("vec_sb", vec)
         gain_sb = load_columns("gain_sb", gain)
-        load_gate(wg1_sb, wg1, 2, 4)
 
+        wg2_turned = turn_gate("wg2_turned", wg2_rows, "x_rows0", nc.vector.tensor_copy, 6)
+        deal_gate(wg2_sb, wg2_turned, 0, 7)
         v2 = (None, gather_scales("v2_s", tab2_s, 0, idx2))
         v2 = (gather_words("v2_w", tab2_w, idx2), v2[1])
         w3_q = [quantize("w3_q0", round_weight("w3_r0", w3_raw0, "round0"), "codes0")]
@@ -177,25 +202,36 @@ def tile_list_fencing_referee_features_kernel(
             w2_s_raw[:].rearrange("p (g q t) -> p g t q", t=PACK, q=P),
         )
 
+        h2_tag = ["small0", "small1", "small2", "small3", "left2", "left3", "codes4", "codes5"]
+
         def put_right(i):
             b, t = divmod(i, PACK)
-            bank = next_bank()
+            bank = next_bank(t)
             mx(bank[:], fp8_cols(w3_q[b], t * P, P), fp8_cols(v2, 0, S), True, True)
-            h2 = tile("h2_%d" % i, [P, S], F32, "small%d" % t)
+            h2 = tile("h2_%d" % i, [P, S], F32, h2_tag[i])
             nc.scalar.activation(h2[:], bank[:], ACT.Square)
+            if b == 1:
+                deal_gate(wg1_sb, wg1_turned, t, t)
+            elif t + 1 < PACK:
+                deal_gate(wg2_sb, wg2_turned, t + 1, t)
             nc.vector.tensor_tensor(pages[i][:].indirect(idx4[:]), h2[:], wg2_sb[:, t, :], MULT)
 
-        for i in range(3):
-            put_right(i)
+        put_right(0)
+        put_right(1)
         w3_q.append(quantize("w3_q1", round_weight("w3_r1", w3_raw1, "round1"), "codes1"))
+        put_right(2)
+        put_right(3)
+        wg1_turned = turn_gate("wg1_turned", wg1_rows, "x_rows0", nc.scalar.copy, 4)
         w1_raw01 = load_weight("w1_raw01", w1, 0, 1, "stage0")
         w1_raw11 = load_weight("w1_raw11", w1, 1, 1, "stage1")
         w4_s = load_scale_rows("w4_s", w4_scales)
         w4_w = load_packed_words("w4_w", w4_words)
-        put_right(3)
         put_right(4)
-        v = [(gather_words("v_w0", tab_w0, idx), gather_scales("v_s0", tab_s, 0, idx))]
-        v.append((gather_words("v_w1", tab_w1, idx), gather_scales("v_s1", tab_s, 1, idx)))
+        v_s0 = gather_scales("v_s0", tab_s, 0, idx)
+        v_s1 = tile("v_s1", [P, S], U8)
+        nc.gpsimd.memset(v_s1[:].bitcast(I32), 0)
+        nc.gpsimd.dma_start(out=v_s1[0:100, :].bitcast(I32), in_=v_s0[4:104, :].bitcast(I32))
+        v = [(gather_words("v_w0", tab_w0, idx), v_s0), (gather_words("v_w1", tab_w1, idx), v_s1)]
         put_right(5)
         w1_q = {}
         w1_q[0, 0] = quantize("w1_q00", round_weight("w1_r00", w1_raw00, "round0"), "codes2")

@@ -256,55 +256,59 @@ def tile_list_fencing_referee_features_kernel(
                 nc.scalar.activation(left2[:, u, :], bank[:], ACT.Identity, bias=1.0)
             return left, left2
 
-        def left_features(pair):
+        def side_features(name, pair, count):
+            dst = tile(name, [P, count, S], F32, "round0")
             left, left2 = products[pair]
-            nc.vector.tensor_tensor(left[:], left[:], left2, MULT)
+            nc.gpsimd.tensor_tensor(dst[:], left[:, 0:count, :], left2[:, 0:count, :], MULT)
+            return dst
 
         def put_left(i, h1):
             nc.vector.tensor_tensor(pages[i][:].indirect(idx3[:]), h1, wg1_sb[:, i % PACK, :], MULT)
 
-        def put_pair(pair):
+        def put_pair(pair, h1):
             for u in range(2):
-                put_left(2 * pair + u, products[pair][0][:, u, :])
+                put_left(2 * pair + u, h1[:, u, :])
 
-        got_tag = ["got0", "got1", "stage1", "round1", "stage0", "left0", "left1", "got0"]
+        got_tag = ["stage0", "stage1", "got0", "got1", "stage0", "left0", "left1", "got0"]
         x_rows = [tile("x_rows0", [P, PACK, PICK], BF16), None]
         chunks = PICK // CHUNK
 
-        def fetch(i):
-            got = tile("got%d" % i, [P, PICK], F32, got_tag[i])
-            nc.vector.tensor_copy(got[:], pages[i][:].indirect(idx5[:]))
+        def fetch(i, got):
+            nc.vector.tensor_copy(got, pages[i][:].indirect(idx5[:]))
             bent = tile("bent%d" % i, [P, PICK], F32, "bent")
-            nc.scalar.activation(bent[:], got[:], ACT.Tanh, bias=vec_sb[:, i : i + 1])
+            nc.scalar.activation(bent[:], got, ACT.Tanh, bias=vec_sb[:, i : i + 1])
             return bent
 
         def fetch_rows(i):
             b, t = divmod(i, PACK)
-            nc.scalar.activation(x_rows[b][:, t, :], fetch(i)[:], ACT.Copy, scale=gain_sb[:, i : i + 1])
+            got = tile("got%d" % i, [P, PICK], F32, got_tag[i])
+            nc.scalar.activation(x_rows[b][:, t, :], fetch(i, got[:])[:], ACT.Copy, scale=gain_sb[:, i : i + 1])
 
         products = [left_products(0), left_products(1)]
-        left_features(0)
-        put_pair(0)
-        left_features(1)
-        fetch_rows(0)
-        fetch_rows(1)
-        put_pair(1)
+        left, left2 = products[0]
+        nc.vector.tensor_tensor(left[:], left[:], left2, MULT)
+        put_pair(0, left)
         w1_q[0, 1] = quantize("w1_q01", round_weight("w1_r01", w1_raw01, "round0"), "codes4")
+        h1_pair = side_features("h1_pair1", 1, 2)
         w1_q[1, 1] = quantize("w1_q11", round_weight("w1_r11", w1_raw11, "round1"), "codes5")
         products.append(left_products(2))
         products.append(left_products(3))
+        fetch_rows(0)
+        fetch_rows(1)
+        put_pair(1, h1_pair)
+        h1_pair = side_features("h1_pair2", 2, 2)
         fetch_rows(2)
         fetch_rows(3)
         woven = []
         for half in range(2):
-            dst = tile("x_woven0%d" % half, [P, PACK * 512], BF16, "round%d" % half)
+            dst = tile("x_woven0%d" % half, [P, PACK * 512], BF16, ["stage3", "stage1"][half])
             nc.scalar.copy(
                 dst[:].rearrange("p (c i t) -> p c t i", i=4, t=PACK),
                 x_rows[0][:, :, half * 512 : (half + 1) * 512].rearrange("p t (c i) -> p c t i", i=4),
             )
             woven.append(dst)
-        left_features(2)
-        put_pair(2)
+        put_pair(2, h1_pair)
+        h1_6 = side_features("h1_6", 3, 1)
         x_rows[1] = tile("x_rows1", [P, 2, PICK], BF16, "wg2")
         fetch_rows(4)
         fetch_rows(5)
@@ -314,19 +318,18 @@ def tile_list_fencing_referee_features_kernel(
                 woven1[c][:].rearrange("p (j t) -> p j t", t=PACK)[:, :, 0:2],
                 x_rows[1][:, :, c * CHUNK : (c + 1) * CHUNK].rearrange("p t j -> p j t"),
             )
+        put_left(6, h1_6[:, 0, :])
+        x_q0 = [quantize("x_q00", woven[0], "codes0")]
+        late = tile("late", [P, PICK + S], F32, "stage3")
         left, left2 = products[3]
-        nc.vector.tensor_tensor(left[:, 0, :], left[:, 0, :], left2[:, 0, :], MULT)
-        put_left(6, left[:, 0, :])
-        got6 = fetch(6)
+        nc.gpsimd.tensor_tensor(late[:, PICK:], left[:, 1, :], left2[:, 1, :], MULT)
+        bent6 = fetch(6, late[:, :PICK])
         for c in range(chunks):
             nc.scalar.activation(
                 woven1[c][:].rearrange("p (j t) -> p j t", t=PACK)[:, :, 2],
-                got6[:, c * CHUNK : (c + 1) * CHUNK], ACT.Copy, scale=gain_sb[:, 6:7],
+                bent6[:, c * CHUNK : (c + 1) * CHUNK], ACT.Copy, scale=gain_sb[:, 6:7],
             )
-        x_q0 = [quantize("x_q00", woven[0], "codes0")]
-        h1_last = tile("h1_last", [P, S], F32, "round0")
-        nc.vector.tensor_tensor(h1_last[:], left[:, 1, :], left2[:, 1, :], MULT)
-        put_left(7, h1_last[:])
+        put_left(7, late[:, PICK:])
         x_q0.append(quantize("x_q01", woven[1], "codes1"))
 
         def out_passes(chunk, a, x_pair, c0):

@@ -1,22 +1,29 @@
 from contextlib import ExitStack
 
 import concourse.mybir as mybir
-from concourse.masks import make_identity
 
-K, K2, T, S, H, T2, PICK, N = 1024, 512, 2048, 512, 1024, 2048, 1024, 512
-FLOPS = 2 * (K * H * S * 2 + K2 * H * S + H * N * PICK)
+K, K2, T, S, H, T2, PICKS, N = 1024, 512, 2048, 512, 1024, 2048, 1024, 512
+FLOPS = 2 * (2 * K * H * S + K2 * H * S + H * N * PICKS)
 
 F32, BF16 = mybir.dt.float32, mybir.dt.bfloat16
 I32, U32, U16, U8 = mybir.dt.int32, mybir.dt.uint32, mybir.dt.uint16, mybir.dt.uint8
 FP8X4, FP4X4 = mybir.dt.float8_e4m3fn_x4, mybir.dt.float4_e2m1fn_x4
-MULT = mybir.AluOpType.mult
+MULT, ADD, EQUAL = mybir.AluOpType.mult, mybir.AluOpType.add, mybir.AluOpType.is_equal
 ACT = mybir.ActivationFunctionType
 
 P = 128
+QUADRANT = 32
 PACK = 4
 PASS = P * PACK
-CHUNK = 256
-NSUB = 128
+BANK = 512
+BANKS = 8
+ROW_TILES = H // P
+LAST = ROW_TILES - 1
+HALF = PICKS // 2
+CHUNK = T2 // 8
+CHUNKS = PICKS // CHUNK
+NARROW = 128
+LIST_ROWS = 16
 
 
 def tile_list_fencing_referee_features_kernel(
@@ -26,41 +33,44 @@ def tile_list_fencing_referee_features_kernel(
     nc = tc.nc
     with ExitStack() as ctx:
         lists = ctx.enter_context(tc.tile_pool(name="lists", bufs=1))
-        sb = ctx.enter_context(tc.tile_pool(name="sb", bufs=1))
+        sbuf = ctx.enter_context(tc.tile_pool(name="sbuf", bufs=1))
         psum = ctx.enter_context(tc.psum_pool(name="psum", bufs=1))
 
-        def tile(name, shape, dtype, tag=None):
-            return sb.tile(shape, dtype, name=name, tag=tag or name, align_bytes=64)
+        def tile(name, shape, dtype, slot=None):
+            return sbuf.tile(shape, dtype, name=name, tag=slot or name, align_bytes=64)
+
+        banks_taken = []
+
+        def take_bank(number=None):
+            count = len(banks_taken)
+            bank = psum.tile([P, BANK], F32, name="bank%d" % count, tag="bank%d" % (count % BANKS if number is None else number))
+            banks_taken.append(bank)
+            return bank
 
         def load_list(name, src):
             dst = lists.tile(list(src.shape), U16, name=name, tag=name)
             nc.sync.dma_start(dst[:], src)
             return dst
 
-        banks_used = []
-
-        def next_bank(slot=None):
-            n = len(banks_used)
-            bank = psum.tile([P, 512], F32, name="bank%d" % n, tag="bank%d" % (n % 8 if slot is None else slot))
-            banks_used.append(bank)
-            return bank
-
         def load_scale_rows(name, src, queues=(nc.sync, nc.sync)):
             passes, width = src.shape[0], src.shape[2]
             dst = tile(name, [P, passes * width], U8)
-            nc.vector.memset(dst[:].bitcast(I32), 0)
+            nc.gpsimd.memset(dst[:].bitcast(I32), 0)
             for q in range(4):
                 queues[q % 2].dma_start(
-                    out=dst[32 * q : 32 * q + 4, :].bitcast(I32).rearrange("p (a c) -> p a c", a=passes),
+                    out=dst[QUADRANT * q : QUADRANT * q + 4, :].bitcast(I32).rearrange("p (a c) -> p a c", a=passes),
                     in_=src[:, 4 * q : 4 * q + 4, :].bitcast(I32).rearrange("a q c -> q a c"),
                 )
             return dst
 
-        def load_packed_scale_rows(name, src):
+        def load_stacked_scale_rows(name, src):
             dst = tile(name, [P, T], U8)
-            nc.vector.memset(dst[:].bitcast(I32), 0)
+            nc.gpsimd.memset(dst[:].bitcast(I32), 0)
             for q in range(4):
-                nc.sync.dma_start(out=dst[32 * q : 32 * q + 8, :].bitcast(I32), in_=src[:, 4 * q : 4 * q + 4, :].bitcast(I32))
+                nc.sync.dma_start(
+                    out=dst[QUADRANT * q : QUADRANT * q + 8, :].bitcast(I32),
+                    in_=src[:, 4 * q : 4 * q + 4, :].bitcast(I32),
+                )
             return dst
 
         def load_table_words(name, src):
@@ -68,17 +78,17 @@ def tile_list_fencing_referee_features_kernel(
             nc.sync.dma_start(out=dst[:], in_=src.rearrange("p t i -> p (t i)").bitcast(I32))
             return dst
 
-        def load_packed_words(name, src, tag=None):
+        def load_fp4_words(name, src, slot=None):
             passes, width = src.shape[0], src.shape[2]
-            dst = tile(name, [P, passes * width], U8, tag)
+            dst = tile(name, [P, passes * width], U8, slot)
             nc.sync.dma_start(
                 out=dst[:].bitcast(I32).rearrange("p (a c) -> p a c", a=passes),
                 in_=src.bitcast(I32).rearrange("a p c -> p a c"),
             )
             return dst
 
-        def load_weight(name, src, a, b, tag):
-            dst = tile(name, [P, PACK, PASS], F32, tag)
+        def load_weight(name, src, a, b, slot):
+            dst = tile(name, [P, PACK, PASS], F32, slot)
             block = src[a * PASS : (a + 1) * PASS, b * PASS : (b + 1) * PASS]
             nc.sync.dma_start(out=dst[:], in_=block.rearrange("(p j) c -> p j c", j=PACK))
             return dst
@@ -90,288 +100,303 @@ def tile_list_fencing_referee_features_kernel(
             nc.sync.dma_start(out=dst[:], in_=rows[t])
             return dst
 
-        def load_gate(name, src, tag):
-            dst = tile(name, [P, S], F32, tag)
+        def load_gate(name, src, slot):
+            dst = tile(name, [P, S], F32, slot)
             nc.sync.dma_start(out=dst[:], in_=src)
             return dst
 
-        def turn_gate(name, rows, tag, copy, slot):
-            bank = next_bank(slot)
-            for jb in range(S // P):
-                nc.tensor.transpose(bank[:, jb * P : (jb + 1) * P], rows[:, jb * P : (jb + 1) * P], ident[:])
-            turned = tile(name, [P, S // P, PACK * P], F32, tag)
-            for rep in range(PACK):
-                copy(turned[:, :, rep * P : (rep + 1) * P], bank[:].rearrange("p (b r) -> p b r", r=P))
-            return turned
-
-        def deal_gate(dst, turned, t, slot=None):
-            bank = next_bank(slot)
-            for jb in range(S // P):
-                nc.tensor.transpose(bank[:, jb * P : (jb + 1) * P], turned[:, jb, t :: PACK], ident[:])
-            nc.scalar.copy(dst[:, t, :], bank[:])
-
-        def load_columns(name, src):
+        def load_row_values(name, src):
             dst = tile(name, [P, 2, PACK], F32)
             nc.sync.dma_start(out=dst[:], in_=src.rearrange("(b p t) -> p b t", b=2, t=PACK))
             return dst[:].rearrange("p b t -> p (b t)")
+
+        def turn_gate(name, rows, slot, copy, bank_number):
+            bank = take_bank(bank_number)
+            for block in range(S // P):
+                cols = slice(block * P, (block + 1) * P)
+                nc.tensor.transpose(bank[:, cols], rows[:, cols], identity[:])
+            turned = tile(name, [P, S // P, PACK * P], F32, slot)
+            copy(
+                turned[:].rearrange("p b (c r) -> p b c r", r=P),
+                bank[:].rearrange("p (b r) -> p b r", r=P).unsqueeze(2).to_broadcast([P, S // P, PACK, P]),
+            )
+            return turned
+
+        def deal_gate(dst, turned, t, bank_number):
+            bank = take_bank(bank_number)
+            for block in range(S // P):
+                nc.tensor.transpose(bank[:, block * P : (block + 1) * P], turned[:, block, t::PACK], identity[:])
+            nc.scalar.copy(dst[:, t, :], bank[:])
 
         def gather_words(name, window, offsets):
             dst = tile(name, [P, S], U32)
             nc.vector.tensor_copy(dst[:], window[:].bitcast(U32).indirect(offsets[:]))
             return dst
 
-        def gather_scales(name, window, a, offsets):
+        def gather_scales(name, window, offsets):
             dst = tile(name, [P, S], U8)
-            nc.vector.tensor_copy(dst[:], window[:, a * T : (a + 1) * T].indirect(offsets[:]))
+            nc.vector.tensor_copy(dst[:], window[:].indirect(offsets[:]))
             return dst
 
-        def round_weight(name, raw, tag):
-            dst = tile(name, [P, PACK * PASS], BF16, tag)
-            nc.scalar.activation(
-                dst[:].rearrange("p (t m j) -> p m j t", t=PACK, j=PACK),
-                raw[:].rearrange("p j (m t) -> p m j t", t=PACK),
-                ACT.Copy,
-            )
-            return dst
-
-        def quantize(name, src, tag=None):
+        def quantize(name, src, slot):
             width = src.shape[1] // PACK
-            codes = tile(name + "_codes", [P, width], U32, tag)
+            codes = tile(name + "_codes", [P, width], U32, slot)
             scales = tile(name + "_scales", [P, width], U8)
             nc.vector.quantize_mx(out=codes[:].bitcast(FP8X4), scales=scales[:], in_=src[:])
             return codes, scales
 
-        def fp8_cols(pair, c0, width):
-            return pair[0][:, c0 : c0 + width].bitcast(FP8X4), pair[1][:, c0 : c0 + width]
+        def quantize_weight(name, raw, rounded_slot, codes_slot):
+            rounded = tile(name + "_rounded", [P, PACK * PASS], BF16, rounded_slot)
+            nc.scalar.activation(
+                rounded[:].rearrange("p (t m j) -> p m j t", t=PACK, j=PACK),
+                raw[:].rearrange("p j (m t) -> p m j t", t=PACK),
+                ACT.Copy,
+            )
+            return quantize(name, rounded, codes_slot)
 
-        def fp4_cols(pair, c0, width):
-            return pair[0][:, 2 * c0 : 2 * (c0 + width)].bitcast(FP4X4), pair[1][:, c0 : c0 + width]
+        def deal_columns(dst, src):
+            nc.vector.tensor_copy(
+                dst.rearrange("p (g t m) -> p g t m", t=PACK, m=P),
+                src.rearrange("p (g m t) -> p g t m", t=PACK, m=P),
+            )
 
-        def mx(dst, lhs, rhs, start, stop):
-            nc.tensor.matmul_mx(out=dst, lhsT=lhs[0], lhsT_scale=lhs[1], rhs=rhs[0], rhs_scale=rhs[1], start=start, stop=stop)
+        def fp8_cols(operand, first, width):
+            return operand[0][:, first : first + width].bitcast(FP8X4), operand[1][:, first : first + width]
 
+        def fp4_cols(operand, first, width):
+            return operand[0][:, 2 * first : 2 * (first + width)].bitcast(FP4X4), operand[1][:, first : first + width]
 
-        pages = [None] * 8
-        wg1_sb = tile("wg1_sb", [P, PACK, S], F32)
-        wg2_sb = tile("wg2_sb", [P, PACK, S], F32, "wg2")
-        ident = tile("ident", [P, P], F32)
-        make_identity(nc, ident[:])
-        wg2_rows = load_gate("wg2_rows", wg2, "got0")
+        def mx(dst, stationary, moving, start, stop):
+            nc.tensor.matmul_mx(
+                out=dst, lhsT=stationary[0], lhsT_scale=stationary[1], rhs=moving[0], rhs_scale=moving[1], start=start, stop=stop
+            )
+
+        gate1 = tile("gate1", [P, PACK, S], F32)
+        gate2 = tile("gate2", [P, PACK, S], F32)
+
+        ones = tile("ones", [P, QUADRANT], F32)
+        nc.vector.memset(ones[:], 1.0)
+        identity = tile("identity", [P, P], F32)
+        nc.vector.memset(identity[:], 0.0)
+        ramp = tile("ramp", [P, QUADRANT], F32)
+        nc.vector.tensor_tensor_scan(ramp[:], ones[:], ones[:], 0.0, MULT, ADD)
+        ramp_turned = tile("ramp_turned", [P, QUADRANT], F32)
+        nc.vector.transpose(ramp_turned[:], ramp[:])
+        for q in range(4):
+            part = slice(QUADRANT * q, QUADRANT * (q + 1))
+            nc.vector.tensor_tensor(identity[part, part], ramp[part, :], ramp_turned[part, :], EQUAL)
+
+        pages = [None] * ROW_TILES
+        wg2_rows = load_gate("wg2_rows", wg2, "picked0")
         idx2 = load_list("idx2", offs2)
-        w3_raw0 = load_weight("w3_raw0", w3, 0, 0, "stage0")
+        w3_raw0 = load_weight("w3_raw0", w3, 0, 0, "wide0")
         tab2_s = load_scale_rows("tab2_s", tab2_scales, (nc.sync, nc.scalar))
         tab2_w = load_table_words("tab2_w", tab2_words[0])
-        w2_w_raw = load_packed_words("w2_w_raw", w2_words, "bent")
+        w2_w_raw = load_fp4_words("w2_w_raw", w2_words, "tanh")
         idx4 = load_list("idx4", offs4)
-        pages[0] = load_page(0)
-        pages[1] = load_page(1)
-        pages[2] = load_page(2)
-        w3_raw1 = load_weight("w3_raw1", w3, 0, 1, "stage1")
-        wg1_rows = load_gate("wg1_rows", wg1, "got1")
+        for i in (0, 1, 2):
+            pages[i] = load_page(i)
+        w3_raw1 = load_weight("w3_raw1", w3, 0, 1, "wide1")
+        wg1_rows = load_gate("wg1_rows", wg1, "picked1")
         pages[3] = load_page(3)
         w2_s_raw = load_scale_rows("w2_s_raw", w2_scales)
         pages[4] = load_page(4)
         idx = load_list("idx", offs)
-        tab_s = load_packed_scale_rows("tab_s", tab_scales)
+        tab_s = load_stacked_scale_rows("tab_s", tab_scales)
         tab_w0 = load_table_words("tab_w0", tab_words[0])
-        w1_raw00 = load_weight("w1_raw00", w1, 0, 0, "stage2")
         pages[5] = load_page(5)
-        w1_raw10 = load_weight("w1_raw10", w1, 1, 0, "stage3")
+        w1_raw00 = load_weight("w1_raw00", w1, 0, 0, "wide2")
+        pages[6] = load_page(6)
+        w1_raw10 = load_weight("w1_raw10", w1, 1, 0, "wide3")
         tab_w1 = load_table_words("tab_w1", tab_words[1])
         idx3 = load_list("idx3", offs3)
-        pages[6] = load_page(6)
         pages[7] = load_page(7)
         idx5 = load_list("idx5", offs5)
-        vec_sb = load_columns("vec_sb", vec)
-        gain_sb = load_columns("gain_sb", gain)
+        vec_sb = load_row_values("vec_sb", vec)
+        gain_sb = load_row_values("gain_sb", gain)
 
         wg2_turned = turn_gate("wg2_turned", wg2_rows, "x_rows0", nc.vector.tensor_copy, 6)
-        deal_gate(wg2_sb, wg2_turned, 0, 7)
-        v2 = (None, gather_scales("v2_s", tab2_s, 0, idx2))
-        v2 = (gather_words("v2_w", tab2_w, idx2), v2[1])
-        w3_q = [quantize("w3_q0", round_weight("w3_r0", w3_raw0, "round0"), "codes0")]
+        deal_gate(gate2, wg2_turned, 0, 7)
+        v2_s = gather_scales("v2_s", tab2_s, idx2)
+        v2 = (gather_words("v2_w", tab2_w, idx2), v2_s)
+        w3_q = [quantize_weight("w3_q0", w3_raw0, "half0", "codes0")]
+        w2 = (tile("w2_w", [P, 2 * 2 * H], U8), tile("w2_s", [P, 2 * H], U8))
+        deal_columns(w2[0][:].bitcast(U16), w2_w_raw[:].bitcast(U16))
+        deal_columns(w2[1][:], w2_s_raw[:])
 
-        w2_w = tile("w2_w", [P, 2 * 2 * H], U8)
-        nc.vector.tensor_copy(
-            w2_w[:].bitcast(U16).rearrange("p (g t q) -> p g t q", t=PACK, q=P),
-            w2_w_raw[:].bitcast(U16).rearrange("p (g q t) -> p g t q", t=PACK, q=P),
-        )
-        w2_s = tile("w2_s", [P, 2 * H], U8)
-        nc.vector.tensor_copy(
-            w2_s[:].rearrange("p (g t q) -> p g t q", t=PACK, q=P),
-            w2_s_raw[:].rearrange("p (g q t) -> p g t q", t=PACK, q=P),
-        )
-
-        h2_tag = ["small0", "small1", "small2", "small3", "left2", "left3", "codes4", "codes5"]
+        h2_slot = ["small0", "small1", "small2", "small3", "pair2", "pair3", "codes4", "codes5"]
 
         def put_right(i):
             b, t = divmod(i, PACK)
-            bank = next_bank(t)
+            bank = take_bank(t)
             mx(bank[:], fp8_cols(w3_q[b], t * P, P), fp8_cols(v2, 0, S), True, True)
-            h2 = tile("h2_%d" % i, [P, S], F32, h2_tag[i])
+            h2 = tile("h2_%d" % i, [P, S], F32, h2_slot[i])
             nc.scalar.activation(h2[:], bank[:], ACT.Square)
             if b == 1:
-                deal_gate(wg1_sb, wg1_turned, t, t)
+                deal_gate(gate1, wg1_turned, t, t)
             elif t + 1 < PACK:
-                deal_gate(wg2_sb, wg2_turned, t + 1, t)
-            nc.vector.tensor_tensor(pages[i][:].indirect(idx4[:]), h2[:], wg2_sb[:, t, :], MULT)
+                deal_gate(gate2, wg2_turned, t + 1, t)
+            nc.vector.tensor_tensor(pages[i][:].indirect(idx4[:]), h2[:], gate2[:, t, :], MULT)
 
         put_right(0)
         put_right(1)
-        w3_q.append(quantize("w3_q1", round_weight("w3_r1", w3_raw1, "round1"), "codes1"))
+        w3_q.append(quantize_weight("w3_q1", w3_raw1, "half1", "codes1"))
         put_right(2)
         put_right(3)
         wg1_turned = turn_gate("wg1_turned", wg1_rows, "x_rows0", nc.scalar.copy, 4)
-        w1_raw01 = load_weight("w1_raw01", w1, 0, 1, "stage0")
-        w1_raw11 = load_weight("w1_raw11", w1, 1, 1, "stage1")
+        w1_raw01 = load_weight("w1_raw01", w1, 0, 1, "wide0")
+        w1_raw11 = load_weight("w1_raw11", w1, 1, 1, "wide1")
         w4_s = load_scale_rows("w4_s", w4_scales)
-        w4_w = load_packed_words("w4_w", w4_words)
+        w4 = (load_fp4_words("w4_w", w4_words), w4_s)
         put_right(4)
-        v_s0 = gather_scales("v_s0", tab_s, 0, idx)
+        v_s0 = gather_scales("v_s0", tab_s, idx)
         v_s1 = tile("v_s1", [P, S], U8)
         nc.gpsimd.memset(v_s1[:].bitcast(I32), 0)
         nc.gpsimd.dma_start(out=v_s1[0:100, :].bitcast(I32), in_=v_s0[4:104, :].bitcast(I32))
         v = [(gather_words("v_w0", tab_w0, idx), v_s0), (gather_words("v_w1", tab_w1, idx), v_s1)]
         put_right(5)
         w1_q = {}
-        w1_q[0, 0] = quantize("w1_q00", round_weight("w1_r00", w1_raw00, "round0"), "codes2")
+        w1_q[0, 0] = quantize_weight("w1_q00", w1_raw00, "half0", "codes2")
         put_right(6)
-        w1_q[1, 0] = quantize("w1_q10", round_weight("w1_r10", w1_raw10, "round1"), "codes3")
+        w1_q[1, 0] = quantize_weight("w1_q10", w1_raw10, "half1", "codes3")
         put_right(7)
 
-        left2_all = [tile("left2_b%d" % b, [P, PACK, S], F32, ["stage3", "stage2"][b]) for b in range(2)]
+        left2_plus1 = [tile("left2_plus1_%d" % b, [P, PACK, S], F32, ["wide3", "wide2"][b]) for b in range(2)]
 
         def left_products(pair):
-            left = tile("left%d" % pair, [P, 2, S], F32, "left%d" % pair)
-            left2 = left2_all[pair // 2][:, 2 * (pair % 2) : 2 * (pair % 2) + 2, :]
+            left = tile("left%d" % pair, [P, 2, S], F32, "pair%d" % pair)
+            factor = left2_plus1[pair // 2][:, 2 * (pair % 2) : 2 * (pair % 2) + 2, :]
             for u in range(2):
                 b, t = divmod(2 * pair + u, PACK)
-                bank = next_bank()
+                bank = take_bank()
                 for a in range(2):
                     mx(bank[:], fp8_cols(w1_q[a, b], t * P, P), fp8_cols(v[a], 0, S), a == 0, a == 1)
                 nc.scalar.copy(left[:, u, :], bank[:])
-                bank = next_bank()
+                bank = take_bank()
                 for a in range(2):
-                    mx(bank[:], fp4_cols((w2_w, w2_s), a * H + b * PASS + t * P, P), fp8_cols(v[a], 0, S), a == 0, a == 1)
-                nc.scalar.activation(left2[:, u, :], bank[:], ACT.Identity, bias=1.0)
-            return left, left2
+                    mx(bank[:], fp4_cols(w2, a * H + b * PASS + t * P, P), fp8_cols(v[a], 0, S), a == 0, a == 1)
+                nc.scalar.activation(factor[:, u, :], bank[:], ACT.Identity, bias=1.0)
+            return left, factor
 
-        def side_features(name, pair, count):
-            dst = tile(name, [P, count, S], F32, "round0")
-            left, left2 = products[pair]
-            nc.gpsimd.tensor_tensor(dst[:], left[:, 0:count, :], left2[:, 0:count, :], MULT)
-            return dst
+        def features_on_gpsimd(name, pair, count):
+            h1 = tile(name, [P, count, S], F32, "half0")
+            left, factor = products[pair]
+            nc.gpsimd.tensor_tensor(h1[:], left[:, 0:count, :], factor[:, 0:count, :], MULT)
+            return h1
 
         def put_left(i, h1):
-            nc.vector.tensor_tensor(pages[i][:].indirect(idx3[:]), h1, wg1_sb[:, i % PACK, :], MULT)
+            nc.vector.tensor_tensor(pages[i][:].indirect(idx3[:]), h1, gate1[:, i % PACK, :], MULT)
 
-        def put_pair(pair, h1):
+        def put_left_pair(pair, h1):
             for u in range(2):
                 put_left(2 * pair + u, h1[:, u, :])
 
-        got_tag = ["stage0", "stage1", "got0", "got1", "stage0", "left0", "left1", "got0"]
-        x_rows = [tile("x_rows0", [P, PACK, PICK], BF16), None]
-        chunks = PICK // CHUNK
+        picked_slot = ["wide0", "wide1", "picked0", "picked1", "wide0", "pair0"]
+        x_rows = [tile("x_rows0", [P, PACK, PICKS], BF16), None]
 
-        def fetch(i, got):
-            nc.vector.tensor_copy(got, pages[i][:].indirect(idx5[:]))
-            bent = tile("bent%d" % i, [P, PICK], F32, "bent")
-            nc.scalar.activation(bent[:], got, ACT.Tanh, bias=vec_sb[:, i : i + 1])
+        def fetch_tanh(i, picked):
+            nc.vector.tensor_copy(picked, pages[i][:].indirect(idx5[:]))
+            bent = tile("tanh%d" % i, [P, PICKS], F32, "tanh")
+            nc.scalar.activation(bent[:], picked, ACT.Tanh, bias=vec_sb[:, i : i + 1])
             return bent
 
         def fetch_rows(i):
             b, t = divmod(i, PACK)
-            got = tile("got%d" % i, [P, PICK], F32, got_tag[i])
-            nc.scalar.activation(x_rows[b][:, t, :], fetch(i, got[:])[:], ACT.Copy, scale=gain_sb[:, i : i + 1])
+            picked = tile("picked_%d" % i, [P, PICKS], F32, picked_slot[i])
+            nc.scalar.activation(x_rows[b][:, t, :], fetch_tanh(i, picked[:])[:], ACT.Copy, scale=gain_sb[:, i : i + 1])
+
+        def word_view(woven):
+            return woven[:].rearrange("p (j t) -> p j t", t=PACK)
+
+        def chunk_cols(c):
+            return slice(c * CHUNK, (c + 1) * CHUNK)
 
         products = [left_products(0), left_products(1)]
-        left, left2 = products[0]
-        nc.vector.tensor_tensor(left[:], left[:], left2, MULT)
-        put_pair(0, left)
-        w1_q[0, 1] = quantize("w1_q01", round_weight("w1_r01", w1_raw01, "round0"), "codes4")
-        h1_pair = side_features("h1_pair1", 1, 2)
-        w1_q[1, 1] = quantize("w1_q11", round_weight("w1_r11", w1_raw11, "round1"), "codes5")
+        left, factor = products[0]
+        nc.vector.tensor_tensor(left[:], left[:], factor, MULT)
+        put_left_pair(0, left)
+        w1_q[0, 1] = quantize_weight("w1_q01", w1_raw01, "half0", "codes4")
+        h1_pair = features_on_gpsimd("h1_pair1", 1, 2)
+        w1_q[1, 1] = quantize_weight("w1_q11", w1_raw11, "half1", "codes5")
         products.append(left_products(2))
         products.append(left_products(3))
         fetch_rows(0)
         fetch_rows(1)
-        put_pair(1, h1_pair)
-        h1_pair = side_features("h1_pair2", 2, 2)
+        put_left_pair(1, h1_pair)
+        h1_pair = features_on_gpsimd("h1_pair2", 2, 2)
         fetch_rows(2)
         fetch_rows(3)
-        woven = []
+
+        woven0 = []
         for half in range(2):
-            dst = tile("x_woven0%d" % half, [P, PACK * 512], BF16, ["stage3", "stage1"][half])
+            dst = tile("woven0_%d" % half, [P, PACK * HALF], BF16, ["wide3", "wide1"][half])
             nc.scalar.copy(
                 dst[:].rearrange("p (c i t) -> p c t i", i=4, t=PACK),
-                x_rows[0][:, :, half * 512 : (half + 1) * 512].rearrange("p t (c i) -> p c t i", i=4),
+                x_rows[0][:, :, half * HALF : (half + 1) * HALF].rearrange("p t (c i) -> p c t i", i=4),
             )
-            woven.append(dst)
-        put_pair(2, h1_pair)
-        h1_6 = side_features("h1_6", 3, 1)
-        x_rows[1] = tile("x_rows1", [P, 2, PICK], BF16, "wg2")
+            woven0.append(dst)
+
+        put_left_pair(2, h1_pair)
+        h1_6 = features_on_gpsimd("h1_6", 3, 1)
+
+        x_rows[1] = tile("x_rows1", [P, 2, PICKS], BF16, "gate2")
         fetch_rows(4)
         fetch_rows(5)
-        woven1 = [tile("x_woven1%d" % c, [P, PACK * CHUNK], BF16, "small%d" % c) for c in range(chunks)]
-        for c in range(chunks):
-            nc.scalar.copy(
-                woven1[c][:].rearrange("p (j t) -> p j t", t=PACK)[:, :, 0:2],
-                x_rows[1][:, :, c * CHUNK : (c + 1) * CHUNK].rearrange("p t j -> p j t"),
-            )
+        woven1 = [tile("woven1_%d" % c, [P, PACK * CHUNK], BF16, "small%d" % c) for c in range(CHUNKS)]
+        for c in range(CHUNKS):
+            nc.scalar.copy(word_view(woven1[c])[:, :, 0:2], x_rows[1][:, :, chunk_cols(c)].rearrange("p t j -> p j t"))
         put_left(6, h1_6[:, 0, :])
-        x_q0 = [quantize("x_q00", woven[0], "codes0")]
-        late = tile("late", [P, PICK + S], F32, "stage3")
-        left, left2 = products[3]
-        nc.gpsimd.tensor_tensor(late[:, PICK:], left[:, 1, :], left2[:, 1, :], MULT)
-        bent6 = fetch(6, late[:, :PICK])
-        for c in range(chunks):
-            nc.scalar.activation(
-                woven1[c][:].rearrange("p (j t) -> p j t", t=PACK)[:, :, 2],
-                bent6[:, c * CHUNK : (c + 1) * CHUNK], ACT.Copy, scale=gain_sb[:, 6:7],
-            )
-        put_left(7, late[:, PICK:])
-        x_q0.append(quantize("x_q01", woven[1], "codes1"))
+        x0 = [quantize("x0_0", woven0[0], "codes0")]
+        late = tile("late", [P, PICKS + S], F32, "wide3")
+        left, factor = products[3]
+        nc.gpsimd.tensor_tensor(late[:, PICKS:], left[:, 1, :], factor[:, 1, :], MULT)
+        tanh6 = fetch_tanh(6, late[:, :PICKS])
+        for c in range(CHUNKS):
+            nc.scalar.activation(word_view(woven1[c])[:, :, 2], tanh6[:, chunk_cols(c)], ACT.Copy, scale=gain_sb[:, 6:7])
+        put_left(LAST, late[:, PICKS:])
+        x0.append(quantize("x0_1", woven0[1], "codes1"))
 
-        def out_passes(chunk, a, x_pair, c0):
-            for nt in range(N // P):
-                bank = out_banks[2 * chunk + nt // 2]
-                for s in range(CHUNK // NSUB):
-                    col = (nt % 2) * CHUNK + s * NSUB
-                    first = a == 0 and col == 0
-                    last = a == 1 and col == 512 - NSUB
-                    mx(bank[:, col : col + NSUB], fp4_cols((w4_w, w4_s), a * N + nt * P, P), fp8_cols(x_pair, c0 + s * NSUB, NSUB), first, last)
+        def out_passes(c, a, x_operand, first_col):
+            for n_tile in range(N // P):
+                bank = out_banks[2 * c + n_tile // 2]
+                for s in range(CHUNK // NARROW):
+                    col = (n_tile % 2) * CHUNK + s * NARROW
+                    mx(
+                        bank[:, col : col + NARROW],
+                        fp4_cols(w4, a * N + n_tile * P, P),
+                        fp8_cols(x_operand, first_col + s * NARROW, NARROW),
+                        a == 0 and col == 0,
+                        a == 1 and col == BANK - NARROW,
+                    )
 
-        out_banks = [next_bank() for c in range(2 * chunks)]
-        for c in range(chunks):
-            out_passes(c, 0, x_q0[c // 2], (c % 2) * CHUNK)
+        out_banks = [take_bank() for number in range(2 * CHUNKS)]
+        for c in range(CHUNKS):
+            half, place = divmod(c * CHUNK, HALF)
+            out_passes(c, 0, x0[half], place)
 
-        got = tile("got7", [P, PICK], F32, got_tag[7])
-        bent_last = tile("bent7", [P, PICK], F32, "bent")
+        picked_last = tile("picked_last", [P, PICKS], F32, "picked0")
+        tanh_last = tile("tanh_last", [P, PICKS], F32, "tanh")
+        staged_slot = ["wide0", "wide1", "wide3", "picked1"]
 
         def fetch_last(c):
-            cols = slice(c * CHUNK, (c + 1) * CHUNK)
-            nc.vector.tensor_copy(got[:, cols], pages[7][:].indirect(idx5[:, c * CHUNK // 16 : (c + 1) * CHUNK // 16]))
-            nc.scalar.activation(bent_last[:, cols], got[:, cols], ACT.Tanh, bias=vec_sb[:, 7:8])
+            offsets = idx5[:, c * CHUNK // LIST_ROWS : (c + 1) * CHUNK // LIST_ROWS]
+            nc.vector.tensor_copy(picked_last[:, chunk_cols(c)], pages[LAST][:].indirect(offsets))
+            nc.scalar.activation(tanh_last[:, chunk_cols(c)], picked_last[:, chunk_cols(c)], ACT.Tanh, bias=vec_sb[:, LAST:])
 
         def gain_last(c):
-            nc.vector.tensor_scalar(
-                woven1[c][:].rearrange("p (j t) -> p j t", t=PACK)[:, :, 3],
-                bent_last[:, c * CHUNK : (c + 1) * CHUNK], gain_sb[:, 7:8], None, MULT,
-            )
+            nc.vector.tensor_scalar(word_view(woven1[c])[:, :, 3], tanh_last[:, chunk_cols(c)], gain_sb[:, LAST:], None, MULT)
 
         def finish(c):
-            x_pair = quantize("x_q1%d" % c, woven1[c], "codes%d" % (2 + c))
-            out_passes(c, 1, x_pair, 0)
-            staged = tile("staged%d" % c, [P, N // P, CHUNK], F32, ["stage0", "stage1", "stage3", "got1"][c])
-            for h in range(2):
-                bank = out_banks[2 * c + h]
-                nc.scalar.activation(staged[:, 2 * h : 2 * h + 2, :].rearrange("p n j -> p (n j)"), bank[:], ACT.Abs)
-                rows = out[2 * h * P : (2 * h + 2) * P, c * CHUNK : (c + 1) * CHUNK]
-                nc.sync.dma_start(out=rows.rearrange("(n p) j -> p n j", p=P), in_=staged[:, 2 * h : 2 * h + 2, :])
+            out_passes(c, 1, quantize("x1_%d" % c, woven1[c], "codes%d" % (2 + c)), 0)
+            staged = tile("staged%d" % c, [P, N // P, CHUNK], F32, staged_slot[c])
+            for u in range(2):
+                two_tiles = staged[:, 2 * u : 2 * u + 2, :]
+                nc.scalar.activation(two_tiles.rearrange("p n j -> p (n j)"), out_banks[2 * c + u][:], ACT.Abs)
+                rows = out[2 * u * P : (2 * u + 2) * P, chunk_cols(c)]
+                nc.sync.dma_start(out=rows.rearrange("(n p) j -> p n j", p=P), in_=two_tiles)
 
         steps = (fetch_last, gain_last, finish)
-        for tick in range(chunks + len(steps) - 1):
-            for depth in range(len(steps)):
-                c = tick - depth
-                if 0 <= c < chunks:
-                    steps[depth](c)
+        for tick in range(CHUNKS + len(steps) - 1):
+            for depth, step in enumerate(steps):
+                if 0 <= tick - depth < CHUNKS:
+                    step(tick - depth)

from contextlib import ExitStack

import concourse.mybir as mybir

K, K2, T, S, H, T2, PICKS, N = 1024, 512, 2048, 512, 1024, 2048, 1024, 512
FLOPS = 2 * (2 * K * H * S + K2 * H * S + H * N * PICKS)

F32, BF16 = mybir.dt.float32, mybir.dt.bfloat16
I32, U32, U16, U8 = mybir.dt.int32, mybir.dt.uint32, mybir.dt.uint16, mybir.dt.uint8
FP8X4, FP4X4 = mybir.dt.float8_e4m3fn_x4, mybir.dt.float4_e2m1fn_x4
MULT, ADD, EQUAL = mybir.AluOpType.mult, mybir.AluOpType.add, mybir.AluOpType.is_equal
ACT = mybir.ActivationFunctionType

P = 128
QUADRANT = 32
PACK = 4
PASS = P * PACK
BANK = 512
BANKS = 8
ROW_TILES = H // P
LAST = ROW_TILES - 1
HALF = PICKS // 2
CHUNK = T2 // 8
CHUNKS = PICKS // CHUNK
NARROW = 128
LIST_ROWS = 16


def tile_list_fencing_referee_features_kernel(
    tc, tab_words, tab_scales, offs, tab2_words, tab2_scales, offs2, w1, w2_words, w2_scales,
    w3, page0, offs3, offs4, wg1, wg2, offs5, vec, gain, w4_words, w4_scales, out,
):
    nc = tc.nc
    with ExitStack() as ctx:
        lists = ctx.enter_context(tc.tile_pool(name="lists", bufs=1))
        sbuf = ctx.enter_context(tc.tile_pool(name="sbuf", bufs=1))
        psum = ctx.enter_context(tc.psum_pool(name="psum", bufs=1))

        def tile(name, shape, dtype, slot=None):
            return sbuf.tile(shape, dtype, name=name, tag=slot or name, align_bytes=64)

        banks_taken = []

        def take_bank(number=None):
            count = len(banks_taken)
            bank = psum.tile([P, BANK], F32, name="bank%d" % count, tag="bank%d" % (count % BANKS if number is None else number))
            banks_taken.append(bank)
            return bank

        def load_list(name, src):
            dst = lists.tile(list(src.shape), U16, name=name, tag=name)
            nc.sync.dma_start(dst[:], src)
            return dst

        def load_scale_rows(name, src, queues=(nc.sync, nc.sync)):
            passes, width = src.shape[0], src.shape[2]
            dst = tile(name, [P, passes * width], U8)
            nc.gpsimd.memset(dst[:].bitcast(I32), 0)
            for q in range(4):
                queues[q % 2].dma_start(
                    out=dst[QUADRANT * q : QUADRANT * q + 4, :].bitcast(I32).rearrange("p (a c) -> p a c", a=passes),
                    in_=src[:, 4 * q : 4 * q + 4, :].bitcast(I32).rearrange("a q c -> q a c"),
                )
            return dst

        def load_stacked_scale_rows(name, src):
            dst = tile(name, [P, T], U8)
            nc.gpsimd.memset(dst[:].bitcast(I32), 0)
            for q in range(4):
                nc.sync.dma_start(
                    out=dst[QUADRANT * q : QUADRANT * q + 8, :].bitcast(I32),
                    in_=src[:, 4 * q : 4 * q + 4, :].bitcast(I32),
                )
            return dst

        def load_table_words(name, src):
            dst = tile(name, [P, T], I32)
            nc.sync.dma_start(out=dst[:], in_=src.rearrange("p t i -> p (t i)").bitcast(I32))
            return dst

        def load_fp4_words(name, src, slot=None):
            passes, width = src.shape[0], src.shape[2]
            dst = tile(name, [P, passes * width], U8, slot)
            nc.sync.dma_start(
                out=dst[:].bitcast(I32).rearrange("p (a c) -> p a c", a=passes),
                in_=src.bitcast(I32).rearrange("a p c -> p a c"),
            )
            return dst

        def load_weight(name, src, a, b, slot):
            dst = tile(name, [P, PACK, PASS], F32, slot)
            block = src[a * PASS : (a + 1) * PASS, b * PASS : (b + 1) * PASS]
            nc.sync.dma_start(out=dst[:], in_=block.rearrange("(p j) c -> p j c", j=PACK))
            return dst

        def load_page(i):
            b, t = divmod(i, PACK)
            dst = tile("page%d" % i, [P, T2], F32)
            rows = page0[b * PASS : (b + 1) * PASS, :].rearrange("(p t) c -> t p c", t=PACK)
            nc.sync.dma_start(out=dst[:], in_=rows[t])
            return dst

        def load_gate(name, src, slot):
            dst = tile(name, [P, S], F32, slot)
            nc.sync.dma_start(out=dst[:], in_=src)
            return dst

        def load_row_values(name, src):
            dst = tile(name, [P, 2, PACK], F32)
            nc.sync.dma_start(out=dst[:], in_=src.rearrange("(b p t) -> p b t", b=2, t=PACK))
            return dst[:].rearrange("p b t -> p (b t)")

        def turn_gate(name, rows, slot, copy, bank_number):
            bank = take_bank(bank_number)
            for block in range(S // P):
                cols = slice(block * P, (block + 1) * P)
                nc.tensor.transpose(bank[:, cols], rows[:, cols], identity[:])
            turned = tile(name, [P, S // P, PACK * P], F32, slot)
            copy(
                turned[:].rearrange("p b (c r) -> p b c r", r=P),
                bank[:].rearrange("p (b r) -> p b r", r=P).unsqueeze(2).to_broadcast([P, S // P, PACK, P]),
            )
            return turned

        def deal_gate(dst, turned, t, bank_number):
            bank = take_bank(bank_number)
            for block in range(S // P):
                nc.tensor.transpose(bank[:, block * P : (block + 1) * P], turned[:, block, t::PACK], identity[:])
            nc.scalar.copy(dst[:, t, :], bank[:])

        def gather_words(name, window, offsets):
            dst = tile(name, [P, S], U32)
            nc.vector.tensor_copy(dst[:], window[:].bitcast(U32).indirect(offsets[:]))
            return dst

        def gather_scales(name, window, offsets):
            dst = tile(name, [P, S], U8)
            nc.vector.tensor_copy(dst[:], window[:].indirect(offsets[:]))
            return dst

        def quantize(name, src, slot):
            width = src.shape[1] // PACK
            codes = tile(name + "_codes", [P, width], U32, slot)
            scales = tile(name + "_scales", [P, width], U8)
            nc.vector.quantize_mx(out=codes[:].bitcast(FP8X4), scales=scales[:], in_=src[:])
            return codes, scales

        def quantize_weight(name, raw, rounded_slot, codes_slot):
            rounded = tile(name + "_rounded", [P, PACK * PASS], BF16, rounded_slot)
            nc.scalar.activation(
                rounded[:].rearrange("p (t m j) -> p m j t", t=PACK, j=PACK),
                raw[:].rearrange("p j (m t) -> p m j t", t=PACK),
                ACT.Copy,
            )
            return quantize(name, rounded, codes_slot)

        def deal_columns(dst, src):
            nc.vector.tensor_copy(
                dst.rearrange("p (g t m) -> p g t m", t=PACK, m=P),
                src.rearrange("p (g m t) -> p g t m", t=PACK, m=P),
            )

        def fp8_cols(operand, first, width):
            return operand[0][:, first : first + width].bitcast(FP8X4), operand[1][:, first : first + width]

        def fp4_cols(operand, first, width):
            return operand[0][:, 2 * first : 2 * (first + width)].bitcast(FP4X4), operand[1][:, first : first + width]

        def mx(dst, stationary, moving, start, stop):
            nc.tensor.matmul_mx(
                out=dst, lhsT=stationary[0], lhsT_scale=stationary[1], rhs=moving[0], rhs_scale=moving[1], start=start, stop=stop
            )

        gate1 = tile("gate1", [P, PACK, S], F32)
        gate2 = tile("gate2", [P, PACK, S], F32)

        ones = tile("ones", [P, QUADRANT], F32)
        nc.vector.memset(ones[:], 1.0)
        identity = tile("identity", [P, P], F32)
        nc.vector.memset(identity[:], 0.0)
        ramp = tile("ramp", [P, QUADRANT], F32)
        nc.vector.tensor_tensor_scan(ramp[:], ones[:], ones[:], 0.0, MULT, ADD)
        ramp_turned = tile("ramp_turned", [P, QUADRANT], F32)
        nc.vector.transpose(ramp_turned[:], ramp[:])
        for q in range(4):
            part = slice(QUADRANT * q, QUADRANT * (q + 1))
            nc.vector.tensor_tensor(identity[part, part], ramp[part, :], ramp_turned[part, :], EQUAL)

        pages = [None] * ROW_TILES
        wg2_rows = load_gate("wg2_rows", wg2, "picked0")
        idx2 = load_list("idx2", offs2)
        w3_raw0 = load_weight("w3_raw0", w3, 0, 0, "wide0")
        tab2_s = load_scale_rows("tab2_s", tab2_scales, (nc.sync, nc.scalar))
        tab2_w = load_table_words("tab2_w", tab2_words[0])
        w2_w_raw = load_fp4_words("w2_w_raw", w2_words, "tanh")
        idx4 = load_list("idx4", offs4)
        for i in (0, 1, 2):
            pages[i] = load_page(i)
        w3_raw1 = load_weight("w3_raw1", w3, 0, 1, "wide1")
        wg1_rows = load_gate("wg1_rows", wg1, "picked1")
        pages[3] = load_page(3)
        w2_s_raw = load_scale_rows("w2_s_raw", w2_scales)
        pages[4] = load_page(4)
        idx = load_list("idx", offs)
        tab_s = load_stacked_scale_rows("tab_s", tab_scales)
        tab_w0 = load_table_words("tab_w0", tab_words[0])
        pages[5] = load_page(5)
        w1_raw00 = load_weight("w1_raw00", w1, 0, 0, "wide2")
        pages[6] = load_page(6)
        w1_raw10 = load_weight("w1_raw10", w1, 1, 0, "wide3")
        tab_w1 = load_table_words("tab_w1", tab_words[1])
        idx3 = load_list("idx3", offs3)
        pages[7] = load_page(7)
        idx5 = load_list("idx5", offs5)
        vec_sb = load_row_values("vec_sb", vec)
        gain_sb = load_row_values("gain_sb", gain)

        wg2_turned = turn_gate("wg2_turned", wg2_rows, "x_rows0", nc.vector.tensor_copy, 6)
        deal_gate(gate2, wg2_turned, 0, 7)
        v2_s = gather_scales("v2_s", tab2_s, idx2)
        v2 = (gather_words("v2_w", tab2_w, idx2), v2_s)
        w3_q = [quantize_weight("w3_q0", w3_raw0, "half0", "codes0")]
        w2 = (tile("w2_w", [P, 2 * 2 * H], U8), tile("w2_s", [P, 2 * H], U8))
        deal_columns(w2[0][:].bitcast(U16), w2_w_raw[:].bitcast(U16))
        deal_columns(w2[1][:], w2_s_raw[:])

        h2_slot = ["small0", "small1", "small2", "small3", "pair2", "pair3", "codes4", "codes5"]

        def put_right(i):
            b, t = divmod(i, PACK)
            bank = take_bank(t)
            mx(bank[:], fp8_cols(w3_q[b], t * P, P), fp8_cols(v2, 0, S), True, True)
            h2 = tile("h2_%d" % i, [P, S], F32, h2_slot[i])
            nc.scalar.activation(h2[:], bank[:], ACT.Square)
            if b == 1:
                deal_gate(gate1, wg1_turned, t, t)
            elif t + 1 < PACK:
                deal_gate(gate2, wg2_turned, t + 1, t)
            nc.vector.tensor_tensor(pages[i][:].indirect(idx4[:]), h2[:], gate2[:, t, :], MULT)

        put_right(0)
        put_right(1)
        w3_q.append(quantize_weight("w3_q1", w3_raw1, "half1", "codes1"))
        put_right(2)
        put_right(3)
        wg1_turned = turn_gate("wg1_turned", wg1_rows, "x_rows0", nc.scalar.copy, 4)
        w1_raw01 = load_weight("w1_raw01", w1, 0, 1, "wide0")
        w1_raw11 = load_weight("w1_raw11", w1, 1, 1, "wide1")
        w4_s = load_scale_rows("w4_s", w4_scales)
        w4 = (load_fp4_words("w4_w", w4_words), w4_s)
        put_right(4)
        v_s0 = gather_scales("v_s0", tab_s, idx)
        v_s1 = tile("v_s1", [P, S], U8)
        nc.gpsimd.memset(v_s1[:].bitcast(I32), 0)
        nc.gpsimd.dma_start(out=v_s1[0:100, :].bitcast(I32), in_=v_s0[4:104, :].bitcast(I32))
        v = [(gather_words("v_w0", tab_w0, idx), v_s0), (gather_words("v_w1", tab_w1, idx), v_s1)]
        put_right(5)
        w1_q = {}
        w1_q[0, 0] = quantize_weight("w1_q00", w1_raw00, "half0", "codes2")
        put_right(6)
        w1_q[1, 0] = quantize_weight("w1_q10", w1_raw10, "half1", "codes3")
        put_right(7)

        left2_plus1 = [tile("left2_plus1_%d" % b, [P, PACK, S], F32, ["wide3", "wide2"][b]) for b in range(2)]

        def left_products(pair):
            left = tile("left%d" % pair, [P, 2, S], F32, "pair%d" % pair)
            factor = left2_plus1[pair // 2][:, 2 * (pair % 2) : 2 * (pair % 2) + 2, :]
            for u in range(2):
                b, t = divmod(2 * pair + u, PACK)
                bank = take_bank()
                for a in range(2):
                    mx(bank[:], fp8_cols(w1_q[a, b], t * P, P), fp8_cols(v[a], 0, S), a == 0, a == 1)
                nc.scalar.copy(left[:, u, :], bank[:])
                bank = take_bank()
                for a in range(2):
                    mx(bank[:], fp4_cols(w2, a * H + b * PASS + t * P, P), fp8_cols(v[a], 0, S), a == 0, a == 1)
                nc.scalar.activation(factor[:, u, :], bank[:], ACT.Identity, bias=1.0)
            return left, factor

        def features_on_gpsimd(name, pair, count):
            h1 = tile(name, [P, count, S], F32, "half0")
            left, factor = products[pair]
            nc.gpsimd.tensor_tensor(h1[:], left[:, 0:count, :], factor[:, 0:count, :], MULT)
            return h1

        def put_left(i, h1):
            nc.vector.tensor_tensor(pages[i][:].indirect(idx3[:]), h1, gate1[:, i % PACK, :], MULT)

        def put_left_pair(pair, h1):
            for u in range(2):
                put_left(2 * pair + u, h1[:, u, :])

        picked_slot = ["wide0", "wide1", "picked0", "picked1", "wide0", "pair0"]
        x_rows = [tile("x_rows0", [P, PACK, PICKS], BF16), None]

        def fetch_tanh(i, picked):
            nc.vector.tensor_copy(picked, pages[i][:].indirect(idx5[:]))
            bent = tile("tanh%d" % i, [P, PICKS], F32, "tanh")
            nc.scalar.activation(bent[:], picked, ACT.Tanh, bias=vec_sb[:, i : i + 1])
            return bent

        def fetch_rows(i):
            b, t = divmod(i, PACK)
            picked = tile("picked_%d" % i, [P, PICKS], F32, picked_slot[i])
            nc.scalar.activation(x_rows[b][:, t, :], fetch_tanh(i, picked[:])[:], ACT.Copy, scale=gain_sb[:, i : i + 1])

        def word_view(woven):
            return woven[:].rearrange("p (j t) -> p j t", t=PACK)

        def chunk_cols(c):
            return slice(c * CHUNK, (c + 1) * CHUNK)

        products = [left_products(0), left_products(1)]
        left, factor = products[0]
        nc.vector.tensor_tensor(left[:], left[:], factor, MULT)
        put_left_pair(0, left)
        w1_q[0, 1] = quantize_weight("w1_q01", w1_raw01, "half0", "codes4")
        h1_pair = features_on_gpsimd("h1_pair1", 1, 2)
        w1_q[1, 1] = quantize_weight("w1_q11", w1_raw11, "half1", "codes5")
        products.append(left_products(2))
        products.append(left_products(3))
        fetch_rows(0)
        fetch_rows(1)
        put_left_pair(1, h1_pair)
        h1_pair = features_on_gpsimd("h1_pair2", 2, 2)
        fetch_rows(2)
        fetch_rows(3)

        woven0 = []
        for half in range(2):
            dst = tile("woven0_%d" % half, [P, PACK * HALF], BF16, ["wide3", "wide1"][half])
            nc.scalar.copy(
                dst[:].rearrange("p (c i t) -> p c t i", i=4, t=PACK),
                x_rows[0][:, :, half * HALF : (half + 1) * HALF].rearrange("p t (c i) -> p c t i", i=4),
            )
            woven0.append(dst)

        put_left_pair(2, h1_pair)
        h1_6 = features_on_gpsimd("h1_6", 3, 1)

        x_rows[1] = tile("x_rows1", [P, 2, PICKS], BF16, "gate2")
        fetch_rows(4)
        fetch_rows(5)
        woven1 = [tile("woven1_%d" % c, [P, PACK * CHUNK], BF16, "small%d" % c) for c in range(CHUNKS)]
        for c in range(CHUNKS):
            nc.scalar.copy(word_view(woven1[c])[:, :, 0:2], x_rows[1][:, :, chunk_cols(c)].rearrange("p t j -> p j t"))
        put_left(6, h1_6[:, 0, :])
        x0 = [quantize("x0_0", woven0[0], "codes0")]
        late = tile("late", [P, PICKS + S], F32, "wide3")
        left, factor = products[3]
        nc.gpsimd.tensor_tensor(late[:, PICKS:], left[:, 1, :], factor[:, 1, :], MULT)
        tanh6 = fetch_tanh(6, late[:, :PICKS])
        for c in range(CHUNKS):
            nc.scalar.activation(word_view(woven1[c])[:, :, 2], tanh6[:, chunk_cols(c)], ACT.Copy, scale=gain_sb[:, 6:7])
        put_left(LAST, late[:, PICKS:])
        x0.append(quantize("x0_1", woven0[1], "codes1"))

        def out_passes(c, a, x_operand, first_col):
            for n_tile in range(N // P):
                bank = out_banks[2 * c + n_tile // 2]
                for s in range(CHUNK // NARROW):
                    col = (n_tile % 2) * CHUNK + s * NARROW
                    mx(
                        bank[:, col : col + NARROW],
                        fp4_cols(w4, a * N + n_tile * P, P),
                        fp8_cols(x_operand, first_col + s * NARROW, NARROW),
                        a == 0 and col == 0,
                        a == 1 and col == BANK - NARROW,
                    )

        out_banks = [take_bank() for number in range(2 * CHUNKS)]
        for c in range(CHUNKS):
            half, place = divmod(c * CHUNK, HALF)
            out_passes(c, 0, x0[half], place)

        picked_last = tile("picked_last", [P, PICKS], F32, "picked0")
        tanh_last = tile("tanh_last", [P, PICKS], F32, "tanh")
        staged_slot = ["wide0", "wide1", "wide3", "picked1"]

        def fetch_last(c):
            offsets = idx5[:, c * CHUNK // LIST_ROWS : (c + 1) * CHUNK // LIST_ROWS]
            nc.vector.tensor_copy(picked_last[:, chunk_cols(c)], pages[LAST][:].indirect(offsets))
            nc.scalar.activation(tanh_last[:, chunk_cols(c)], picked_last[:, chunk_cols(c)], ACT.Tanh, bias=vec_sb[:, LAST:])

        def gain_last(c):
            nc.vector.tensor_scalar(word_view(woven1[c])[:, :, 3], tanh_last[:, chunk_cols(c)], gain_sb[:, LAST:], None, MULT)

        def finish(c):
            out_passes(c, 1, quantize("x1_%d" % c, woven1[c], "codes%d" % (2 + c)), 0)
            staged = tile("staged%d" % c, [P, N // P, CHUNK], F32, staged_slot[c])
            for u in range(2):
                two_tiles = staged[:, 2 * u : 2 * u + 2, :]
                nc.scalar.activation(two_tiles.rearrange("p n j -> p (n j)"), out_banks[2 * c + u][:], ACT.Abs)
                rows = out[2 * u * P : (2 * u + 2) * P, chunk_cols(c)]
                nc.sync.dma_start(out=rows.rearrange("(n p) j -> p n j", p=P), in_=two_tiles)

        steps = (fetch_last, gain_last, finish)
        for tick in range(CHUNKS + len(steps) - 1):
            for depth, step in enumerate(steps):
                if 0 <= tick - depth < CHUNKS:
                    step(tick - depth)
